import numpy as np
import ml_dtypes


def mxq(x, axis, fmt="e4m3"):
    dtype, down = {"e4m3": (ml_dtypes.float8_e4m3fn, 7), "e5m2": (ml_dtypes.float8_e5m2, 14)}[fmt]
    v = np.moveaxis(np.asarray(x, np.float32).astype(ml_dtypes.bfloat16).astype(np.float64), axis, -1)
    blocks = v.reshape(v.shape[:-1] + (-1, 32))
    amax = np.abs(blocks).max(-1, keepdims=True)
    byte = np.maximum(np.where(amax > 0, np.frexp(amax)[1] - 1 + 127, 0) - down, 1)
    scale = np.exp2(byte - 127.0)
    codes = (blocks / scale).astype(np.float32).astype(dtype).astype(np.float64)
    return np.moveaxis((codes * scale).reshape(v.shape), -1, axis)


WIDE = False


def mx_kscale(k):
    if not WIDE:
        return np.ones(k)
    levels = np.array([10, -10, 5, -5, 0])
    if k % 512:
        return np.exp2(np.random.permutation(np.resize(levels, k // 32))).repeat(32)
    a = np.empty((k // 512, 16))
    for p in range(k // 512):
        a[p, :8] = np.random.permutation(np.resize(levels, 8))
        for g in range(8):
            far = levels[np.abs(levels - a[p, g]) >= 10]
            a[p, g + 8] = far[np.random.randint(len(far))]
    return np.exp2(a.ravel()).repeat(32)


BF16 = ml_dtypes.bfloat16


def bf(x):
    return np.asarray(x, np.float32).astype(BF16)


def f64(x):
    return np.asarray(x).astype(np.float64)


E2M1 = np.array([0.0, 0.5, 1.0, 1.5, 2.0, 3.0, 4.0, 6.0, -0.0, -0.5, -1.0, -1.5, -2.0, -3.0, -4.0, -6.0])


def pack_weight(w, fmt):
    k, n = w.shape
    w = f64(bf(w)).reshape(k // 32, 32, n)
    amax = np.abs(w).max(1)
    if fmt == "e4m3":
        byte = np.frexp(amax)[1] - 1 + 127 - 7
    else:
        mant, ex = np.frexp(amax / 6.0)
        byte = np.where(mant > 0.5, ex, ex - 1) + 127
    byte = np.clip(np.where(amax > 0, byte, 1), 1, 254)
    scaled = (w * np.exp2(127.0 - byte)[:, None, :]).reshape(k, n).astype(np.float32)
    by_word = np.ascontiguousarray(scaled.reshape(k // 512, 128, 4, n).transpose(0, 1, 3, 2))
    if fmt == "e4m3":
        words = by_word.astype(ml_dtypes.float8_e4m3fn).view(np.uint8)
    else:
        c = by_word.astype(ml_dtypes.float4_e2m1fn).view(np.uint8) & 0xF
        words = c[..., 0::2] | (c[..., 1::2] << 4)
    return np.ascontiguousarray(words), np.ascontiguousarray(byte.astype(np.uint8).reshape(k // 512, 16, n))


def unpack_weight(words, scales, fmt):
    g, p, n, _ = words.shape
    if fmt == "e4m3":
        vals = np.ascontiguousarray(words).view(ml_dtypes.float8_e4m3fn).astype(np.float64)
    else:
        nib = np.empty((g, p, n, 4), np.uint8)
        nib[..., 0::2] = words & 0xF
        nib[..., 1::2] = words >> 4
        vals = E2M1[nib]
    vals = vals * np.repeat(np.exp2(scales.astype(np.float64) - 127.0), 8, axis=1)[..., None]
    return vals.transpose(0, 1, 3, 2).reshape(g * 512, n)


B, D, X = 1024, 1024, 512


def _euler(state, z):
    return state + 0.5 * (np.tanh(z) - 0.5 * state)


def draw0():
    s, t = mx_kscale(X), mx_kscale(D)
    h = bf(np.random.standard_normal((B, D)) * 0.5)
    x = bf(np.random.standard_normal((B, X)) * s)
    w = bf(np.random.standard_normal((D, D)) * np.sqrt(2.0 / D))
    win_words, win_scales = pack_weight(np.random.standard_normal((X, D)) / np.sqrt(X) / s[:, None], "e4m3")
    return {"h": h,
            "x": x,
            "w": w,
            "win_words": win_words,
            "win_scales": win_scales,
            "b": bf(np.random.standard_normal(D) * 0.3),
            "p": bf((1.0 + 0.25 * np.random.standard_normal(D)) * t),
            "r": bf((1.0 + 0.25 * np.random.standard_normal(D)) / t)}


def core(h, x, w, win_words, win_scales, b, p, r):
    h, w, b, p, r = f64(h), f64(w), f64(b), f64(p), f64(r)
    a = mxq(r[:, None] * (w - w.T), 0, "e4m3")
    c = (mxq(f64(x), 1, "e4m3") @ unpack_weight(win_words, win_scales, "e4m3")) + b[None, :]
    z1 = (mxq(h * p[None, :], 1, "e4m3") @ a) + c
    u1 = _euler(h, z1)
    z2 = (mxq(u1 * p[None, :], 1, "e4m3") @ a) + c
    return 0.5 * h + 0.5 * _euler(u1, z2)


def e4m3fn_bytes(y):
    return np.clip(np.asarray(y, np.float64), -448.0, 448.0).astype(np.float32).astype(ml_dtypes.float8_e4m3fn).view(np.uint8)


def e4m3fn_values(b):
    return np.asarray(b, np.uint8).view(ml_dtypes.float8_e4m3fn).astype(np.float64)


def setup_inputs():
    d = draw0()
    x0 = np.asarray(d['x']).astype(np.float64)
    s = (np.max(np.abs(x0), axis=(0,), keepdims=True) / 448.0).astype(np.float32)
    out = {}
    for k, v in d.items():
        if k == 'x':
            out['x_bytes'] = e4m3fn_bytes(x0 / s.astype(np.float64))
            out['x_scale'] = s
        else:
            out[k] = v
    return out


def reference(h, x_bytes, x_scale, w, win_words, win_scales, b, p, r):
    return core(h, e4m3fn_values(x_bytes) * x_scale.astype(np.float64), w, win_words, win_scales, b, p, r)

from contextlib import ExitStack

import concourse.mybir as mybir
from concourse.masks import make_identity

F32 = mybir.dt.float32
BF16 = mybir.dt.bfloat16
I32 = mybir.dt.int32
U32 = mybir.dt.uint32
U8 = mybir.dt.uint8
FP8 = mybir.dt.float8_e4m3fn
FP8X4 = mybir.dt.float8_e4m3fn_x4
ACT = mybir.ActivationFunctionType
ALU = mybir.AluOpType

B, D, X = 1024, 1024, 512
P = 128
PACK = 4
HALF = 512
FLOPS = 2 * 2 * B * D * D + 2 * B * X * D


def tile_antisymmetricssprk2step_w8_kernel(
    tc, h, x_bytes, x_scale, w, win_words, win_scales, b, p, r, out
):
    nc = tc.nc
    with ExitStack() as ctx:
        keep = ctx.enter_context(tc.tile_pool(name="keep", bufs=1))
        work = ctx.enter_context(tc.tile_pool(name="work", bufs=2))
        psum = ctx.enter_context(tc.psum_pool(name="psum", bufs=4))

        h_nat = keep.tile([P, 8, D], BF16, name="h_nat")
        h_half = keep.tile([P, 8, D], BF16, name="h_half")
        w_nat = keep.tile([P, 2, PACK, D], BF16, name="w_nat")
        x_raw = keep.tile([P, 8, X], U8, name="x_raw")
        x_wide = keep.tile([P, 8, X], BF16, name="x_wide")
        wq_raw = keep.tile([P, D], I32, name="wq_raw")
        wq = keep.tile([P, D], I32, name="wq", align_bytes=64)
        ws_raw = keep.tile([P, D], U8, name="ws_raw", align_bytes=64)
        ws = keep.tile([P, D], U8, name="ws", align_bytes=64)
        ident = keep.tile([P, P], F32, name="ident")
        ident_bf = keep.tile([P, P], BF16, name="ident_bf")
        neg_bf = keep.tile([P, P], BF16, name="neg_bf")
        p_bf = keep.tile([P, 2, PACK], BF16, name="p_bf")
        r_bf = keep.tile([P, 2, PACK], BF16, name="r_bf")
        b_bf = keep.tile([P, 2, PACK], BF16, name="b_bf")
        p_half = keep.tile([P, 8], F32, name="p_half")
        r_f = keep.tile([P, 2, PACK], F32, name="r_f")
        b_f = keep.tile([P, 8], F32, name="b_f")
        xs = keep.tile([P, PACK], F32, name="xs")
        warm = keep.tile([P, 1], F32, name="warm")
        hT = [keep.tile([P, 2, HALF, PACK], BF16, name=f"hT{i}") for i in range(2)]
        q = [keep.tile([P, 8, HALF], F32, name=f"q{i}") for i in range(2)]
        hc = [keep.tile([P, 2, HALF], U32, name=f"hc{i}", align_bytes=64) for i in range(2)]
        hs = [keep.tile([P, 2, HALF], U8, name=f"hs{i}", align_bytes=64) for i in range(2)]
        xc = [keep.tile([P, HALF], U32, name=f"xc{i}", align_bytes=64) for i in range(2)]
        xsc = [keep.tile([P, HALF], U8, name=f"xsc{i}", align_bytes=64) for i in range(2)]
        uc = [keep.tile([P, 2, HALF], U32, name=f"uc{i}", align_bytes=64) for i in range(2)]
        us = [keep.tile([P, 2, HALF], U8, name=f"us{i}", align_bytes=64) for i in range(2)]
        ac = [keep.tile([P, 2, P], U32, name=f"ac{i}", align_bytes=64) for i in range(8)]
        asc = [keep.tile([P, 2, P], U8, name=f"asc{i}", align_bytes=64) for i in range(8)]

        xv = x_bytes.rearrange("(p c) k -> p c k", c=8)
        hv = h.rearrange("(p c) n -> p c n", c=8)
        wv = w.rearrange("(g p t) n -> g p t n", g=2, t=PACK)
        ov = out.rearrange("(p c) n -> p c n", c=8)
        nc.vector.memset(ws_raw[:].bitcast(I32), 0)
        nc.vector.memset(warm[:], 0.0)
        nc.scalar.activation(out=warm[:], in_=warm[:], func=ACT.Tanh)
        nc.scalar.dma_start(out=xs[:], in_=x_scale.rearrange("o (p t) -> p (o t)", t=PACK))
        nc.scalar.dma_start(out=p_bf[:], in_=p.rearrange("(g p t) -> p g t", g=2, t=PACK))
        nc.scalar.dma_start(out=r_bf[:], in_=r.rearrange("(g p t) -> p g t", g=2, t=PACK))
        nc.scalar.dma_start(out=b_bf[:], in_=b.rearrange("(g p t) -> p g t", g=2, t=PACK))
        nc.sync.dma_start(out=x_raw[:, 0:4, :], in_=xv[:, 0:4, :])
        nc.sync.dma_start(out=h_nat[:, 0:2, :], in_=hv[:, 0:2, :])
        nc.sync.dma_start(out=h_nat[:, 2:4, :], in_=hv[:, 2:4, :])
        nc.sync.dma_start(out=w_nat[:, 0], in_=wv[0])
        nc.sync.dma_start(out=w_nat[:, 1, :, 0:HALF], in_=wv[1][:, :, 0:HALF])
        for quad in range(4):
            nc.sync.dma_start(
                out=ws_raw[32 * quad : 32 * quad + 4, :].bitcast(I32),
                in_=win_scales[0][4 * quad : 4 * quad + 4, :].bitcast(I32),
            )
        nc.sync.dma_start(out=wq_raw[:], in_=win_words[0].rearrange("p n t -> p (n t)").bitcast(I32))
        nc.sync.dma_start(out=x_raw[:, 4:8, :], in_=xv[:, 4:8, :])
        nc.sync.dma_start(out=w_nat[:, 1, :, HALF:D], in_=wv[1][:, :, HALF:D])
        nc.sync.dma_start(out=h_nat[:, 4:6, :], in_=hv[:, 4:6, :])
        nc.sync.dma_start(out=h_nat[:, 6:8, :], in_=hv[:, 6:8, :])

        make_identity(nc, ident[:])
        make_identity(nc, ident_bf[:])
        nc.vector.tensor_scalar(neg_bf[:], ident_bf[:], -1.0, None, ALU.mult)
        nc.vector.tensor_scalar(p_half[:], p_bf[:].rearrange("p g t -> p (g t)"), 0.5, None, ALU.mult)
        nc.vector.tensor_copy(out=r_f[:], in_=r_bf[:])
        nc.vector.tensor_copy(out=b_f[:], in_=b_bf[:].rearrange("p g t -> p (g t)"))
        def win_columns():
            nc.gpsimd.tensor_copy(
                out=ws[:].rearrange("p (g t m) -> p g t m", g=2, t=PACK),
                in_=ws_raw[:].rearrange("p (g m t) -> p g t m", g=2, t=PACK),
            )
            nc.vector.tensor_copy(
                out=wq[:].rearrange("p (g t m) -> p g t m", g=2, t=PACK),
                in_=wq_raw[:].rearrange("p (g m t) -> p g t m", g=2, t=PACK),
            )

        def bank(tag):
            return psum.tile([P, HALF], F32, name="bank", tag=tag)

        def widen_x(half):
            for c in range(4 * half, 4 * half + 4, 2):
                nc.scalar.copy(out=x_wide[:, c : c + 2, :], in_=x_raw[:, c : c + 2, :].bitcast(FP8))

        xi = {}
        hp = {}
        banks = {}

        def x_turn(half, pair):
            tb = banks["x", half, pair] = bank("t")
            for j in range(2):
                words = x_wide[:, 4 * half + 2 * pair + j, :].bitcast(F32)
                for u in range(2):
                    nc.tensor.transpose(tb[:, 256 * u + P * j : 256 * u + P * (j + 1)], words[:, u::2], ident[:])

        def x_scale_up(half, pair):
            if pair == 0:
                xi[half] = work.tile([P, HALF, PACK], BF16, name="xi", align_bytes=64)
            nc.vector.tensor_tensor(
                out=xi[half][:, 256 * pair : 256 * (pair + 1), :].rearrange("p b (u e) -> p b u e", u=2),
                in0=banks["x", half, pair][:].bitcast(BF16).rearrange("p (u b e) -> p b u e", u=2, e=2),
                in1=xs[:].rearrange("p (u e) -> p u e", u=2).unsqueeze(1).to_broadcast([P, 256, 2, 2]),
                op=ALU.mult,
            )

        def x_quant(half):
            nc.vector.quantize_mx(
                out=xc[half][:].bitcast(FP8X4), scales=xsc[half][:], in_=xi[half][:].rearrange("p b t -> p (b t)")
            )

        def h_turn(half, pair, g):
            tb = banks["h", half, pair, g] = bank("t")
            for j in range(2):
                words = h_nat[:, 4 * half + 2 * pair + j, 512 * g : 512 * (g + 1)].bitcast(F32)
                for u in range(2):
                    nc.tensor.transpose(tb[:, 256 * u + P * j : 256 * u + P * (j + 1)], words[:, u::2], ident[:])

        def h_copy(half, pair, g):
            nc.scalar.copy(
                out=hT[half][:, g, 256 * pair : 256 * (pair + 1), :]
                .rearrange("p b t -> p (b t)")
                .bitcast(F32)
                .rearrange("p (b u) -> p b u", u=2),
                in_=banks["h", half, pair, g][:].rearrange("p (u b) -> p b u", u=2),
            )

        def h_gain(half, g, pair):
            if pair == 0:
                hp[half, g] = work.tile([P, HALF, PACK], BF16, name="hp", align_bytes=64)
            s = slice(256 * pair, 256 * pair + 256)
            nc.vector.tensor_tensor(
                out=hp[half, g][:, s],
                in0=hT[half][:, g, s],
                in1=p_bf[:, g, :].unsqueeze(1).to_broadcast([P, 256, PACK]),
                op=ALU.mult,
            )

        def h_quant(half, g):
            nc.vector.quantize_mx(
                out=hc[half][:, g, :].bitcast(FP8X4),
                scales=hs[half][:, g, :],
                in_=hp[half, g][:].rearrange("p b t -> p (b t)"),
            )

        ab = {}

        def a_mm(c, g):
            go, to = c // PACK, c % PACK
            sb = banks["a", c, g] = bank("t")
            for t in range(PACK):
                nc.tensor.matmul(
                    out=sb[:, P * t : P * (t + 1)],
                    lhsT=ident_bf[:],
                    rhs=w_nat[:, g, t, 512 * go + to : 512 * (go + 1) : PACK],
                    start=True,
                    stop=False,
                )
                nc.tensor.matmul(
                    out=sb[:, P * t : P * (t + 1)],
                    lhsT=w_nat[:, go, to, 512 * g + t : 512 * (g + 1) : PACK],
                    rhs=neg_bf[:],
                    start=False,
                    stop=True,
                )

        def a_gain(c, g):
            if g == 0:
                ab[c] = work.tile([P, 2, P, PACK], BF16, name="ab", bufs=3, align_bytes=64)
            sb = banks["a", c, g]
            if c in A_SPLIT:
                ap = work.tile([P, PACK, P], BF16, name="ap")
                for t in range(PACK):
                    nc.scalar.activation(
                        out=ap[:, t, :], in_=sb[:, P * t : P * (t + 1)], func=ACT.Copy, scale=r_f[:, g, t : t + 1]
                    )
                nc.scalar.copy(out=ab[c][:, g], in_=ap[:].rearrange("p t m -> p m t"))
                return
            nc.vector.tensor_tensor(
                out=ab[c][:, g],
                in0=sb[:].rearrange("p (t m) -> p m t", t=PACK),
                in1=r_f[:, g, :].unsqueeze(1).to_broadcast([P, P, PACK]),
                op=ALU.mult,
            )

        def a_quant(c):
            nc.vector.quantize_mx(
                out=ac[c][:].rearrange("p g m -> p (g m)").bitcast(FP8X4),
                scales=asc[c][:].rearrange("p g m -> p (g m)"),
                in_=ab[c][:].rearrange("p g m t -> p (g m t)"),
            )

        ths = {}

        def product(c, half, second):
            codes, scales = (uc, us) if second else (hc, hs)
            z = banks["z", half, second, c] = bank("z")
            for g in range(2):
                nc.tensor.matmul_mx(
                    out=z[:],
                    lhsT=ac[c][:, g, :].bitcast(FP8X4),
                    lhsT_scale=asc[c][:, g, :],
                    rhs=codes[half][:, g, :].bitcast(FP8X4),
                    rhs_scale=scales[half][:, g, :],
                    start=(g == 0),
                    stop=False,
                )
            nc.tensor.matmul_mx(
                out=z[:],
                lhsT=wq[:, P * c : P * (c + 1)].bitcast(FP8X4),
                lhsT_scale=ws[:, P * c : P * (c + 1)],
                rhs=xc[half][:].bitcast(FP8X4),
                rhs_scale=xsc[half][:],
                start=False,
                stop=True,
            )

        def tanh(c, half, second):
            th = ths[half, second, c] = work.tile([P, HALF], F32, name="th", bufs=6)
            nc.scalar.activation(
                out=th[:], in_=banks["z", half, second, c][:], func=ACT.Tanh, bias=b_f[:, c : c + 1]
            )

        up = {}
        ui = {}

        def q_add(c, half):
            g, t = c // PACK, c % PACK
            nc.vector.scalar_tensor_tensor(
                out=q[half][:, c, :],
                in0=hT[half][:, g, :, t],
                scalar=1.5,
                in1=ths[half, False, c][:],
                op0=ALU.mult,
                op1=ALU.add,
            )

        def u_gain(c, half):
            g, t = c // PACK, c % PACK
            ns = NS[half][g]
            if t == 0:
                up[half, g] = work.tile([P, PACK, HALF], BF16, name="up")
                ui[half, g] = work.tile([P, HALF, PACK], BF16, name="ui", align_bytes=64)
            if ns:
                nc.scalar.activation(
                    out=up[half, g][:, t, 0:ns], in_=q[half][:, c, 0:ns], func=ACT.Copy, scale=p_half[:, c : c + 1]
                )

        def u_weave(half, g):
            ns = NS[half][g]
            if ns < HALF:
                nc.vector.tensor_tensor(
                    out=ui[half, g][:, ns:HALF, :],
                    in0=q[half][:, PACK * g : PACK * (g + 1), ns:HALF].rearrange("p t b -> p b t"),
                    in1=p_half[:, PACK * g : PACK * (g + 1)].unsqueeze(1).to_broadcast([P, HALF - ns, PACK]),
                    op=ALU.mult,
                )
            if ns:
                nc.scalar.copy(
                    out=ui[half, g][:, 0:ns, :], in_=up[half, g][:, :, 0:ns].rearrange("p t b -> p b t")
                )

        def u_quant(half, g):
            nc.vector.quantize_mx(
                out=uc[half][:, g, :].bitcast(FP8X4),
                scales=us[half][:, g, :],
                in_=ui[half, g][:].rearrange("p b t -> p (b t)"),
            )

        ys = {}

        def y_add(c, half):
            g, t = c // PACK, c % PACK
            if t == 0:
                ys[half, g] = work.tile([P, PACK, HALF], F32, name="ys")
            nc.vector.scalar_tensor_tensor(
                out=ys[half, g][:, t, :],
                in0=q[half][:, c, :],
                scalar=0.75,
                in1=ths[half, True, c][:],
                op0=ALU.mult,
                op1=ALU.add,
            )

        def o_turn(half, g, j):
            tb = banks["o", half, g, j] = bank("t")
            for i in range(PACK):
                nc.tensor.transpose(tb[:, P * i : P * (i + 1)], ys[half, g][:, i, P * j : P * (j + 1)], ident[:])

        def o_add(half, g, j):
            row = 4 * half + j
            o = work.tile([P, P, PACK], F32, name="o", bufs=4)
            nc.vector.scalar_tensor_tensor(
                out=o[:],
                in0=banks["o", half, g, j][:].rearrange("p (t m) -> p m t", t=PACK),
                scalar=0.25,
                in1=h_half[:, row, 512 * g : 512 * (g + 1)].rearrange("p (m t) -> p m t", t=PACK),
                op0=ALU.mult,
                op1=ALU.add,
            )
            nc.sync.dma_start(out=ov[:, row, 512 * g : 512 * (g + 1)], in_=o[:].rearrange("p m t -> p (m t)"))

        def halve(half):
            s = slice(4 * half, 4 * half + 4)
            nc.vector.tensor_scalar(h_half[:, s, :], h_nat[:, s, :], 0.5, None, ALU.mult)

        A_SPLIT = (1,3,5)
        NS = ((512,256),(256,256))
        widen_x(0)
        for pair in range(2):
            x_turn(0, pair)
            for g in range(2):
                h_turn(0, pair, g)
                h_copy(0, pair, g)
        for pair in range(2):
            x_scale_up(0, pair)
        for pair in range(2):
            for g in range(2):
                h_gain(0, g, pair)
        x_quant(0)
        h_quant(0, 0)
        h_quant(0, 1)
        widen_x(1)
        win_columns()
        for i in range(12):
            if i < 8:
                a_mm(i, 0)
                a_mm(i, 1)
                a_gain(i, 0)
                a_gain(i, 1)
            if 1 <= i < 9:
                product(i - 1, 0, False)
                tanh(i - 1, 0, False)
            if i in (2, 3):
                x_turn(1, i - 2)
                x_scale_up(1, i - 2)
            if i == 4:
                x_quant(1)
            if i in (5, 6):
                for g in range(2):
                    h_turn(1, i - 5, g)
                    h_copy(1, i - 5, g)
            if i in (6, 7):
                for g in range(2):
                    h_gain(1, g, i - 6)
            if i == 8:
                h_quant(1, 0)
                h_quant(1, 1)
            if 2 <= i < 10:
                q_add(i - 2, 0)
                u_gain(i - 2, 0)
            if i < 8:
                a_quant(i)
            if i == 6 or i == 10:
                u_weave(0, i == 10)
            if i == 7 or i == 11:
                u_quant(0, i == 11)
            if i >= 9:
                product(i - 9, 1, False)
                tanh(i - 9, 1, False)
            if i >= 10:
                q_add(i - 10, 1)
                u_gain(i - 10, 1)
        halve(0)
        for i in range(3, 18):
            if i < 8:
                product(i, 1, False)
                tanh(i, 1, False)
            if i <= 8:
                q_add(i - 1, 1)
                u_gain(i - 1, 1)
            if i in (5, 9):
                u_weave(1, i == 9)
            if i in (6, 10):
                u_quant(1, i == 10)
            k = i - 3
            if k < 8:
                product(k, 0, True)
                tanh(k, 0, True)
            if 1 <= k < 9:
                y_add(k - 1, 0)
            if k in (5, 9):
                for j in range(4):
                    o_turn(0, k == 9, j)
            if k in (6, 10):
                for j in range(4):
                    o_add(0, k == 10, j)
            if k == 5:
                halve(1)
            m = i - 10
            if 0 <= m < 8:
                product(m, 1, True)
                tanh(m, 1, True)
        for c in range(8):
            y_add(c, 1)
            if c % 4 == 3:
                for j in range(4):
                    o_turn(1, c // 4, j)
                for j in range(4):
                    o_add(1, c // 4, j)
